import numpy as np
import ml_dtypes


def mxq(x, axis, fmt="e4m3"):
    dtype, down = {"e4m3": (ml_dtypes.float8_e4m3fn, 7), "e5m2": (ml_dtypes.float8_e5m2, 14)}[fmt]
    v = np.moveaxis(np.asarray(x, np.float32).astype(ml_dtypes.bfloat16).astype(np.float64), axis, -1)
    blocks = v.reshape(v.shape[:-1] + (-1, 32))
    amax = np.abs(blocks).max(-1, keepdims=True)
    byte = np.maximum(np.where(amax > 0, np.frexp(amax)[1] - 1 + 127, 0) - down, 1)
    scale = np.exp2(byte - 127.0)
    codes = (blocks / scale).astype(np.float32).astype(dtype).astype(np.float64)
    return np.moveaxis((codes * scale).reshape(v.shape), -1, axis)


WIDE = False


def mx_kscale(k):
    if not WIDE:
        return np.ones(k)
    levels = np.array([10, -10, 5, -5, 0])
    if k % 512:
        return np.exp2(np.random.permutation(np.resize(levels, k // 32))).repeat(32)
    a = np.empty((k // 512, 16))
    for p in range(k // 512):
        a[p, :8] = np.random.permutation(np.resize(levels, 8))
        for g in range(8):
            far = levels[np.abs(levels - a[p, g]) >= 10]
            a[p, g + 8] = far[np.random.randint(len(far))]
    return np.exp2(a.ravel()).repeat(32)


BF16 = ml_dtypes.bfloat16


def bf(x):
    return np.asarray(x, np.float32).astype(BF16)


def f64(x):
    return np.asarray(x).astype(np.float64)

E4M3FN = np.array([(-1.0 if i & 128 else 1.0) * ((1.0 + (i & 7) / 8.0) * 2.0 ** (((i >> 3) & 15) - 7) if i & 120 else (i & 7) * 2.0 ** -9) for i in range(256)])


def e4m3fn_bytes(y):
    return np.clip(np.asarray(y, np.float64), -448.0, 448.0).astype(np.float32).astype(ml_dtypes.float8_e4m3fn).view(np.uint8)


def e4m3fn_values(b):
    return E4M3FN[b]


M, N, R, BLK = 2048, 1536, 512, 128
KEEP = 0.9


def setup_inputs():
    s, t = mx_kscale(N), mx_kscale(R)
    a = np.random.standard_normal((R, N)) / np.sqrt(N) / s
    b = np.random.standard_normal((R, N)) / np.sqrt(R) / t[:, None]
    d = {"mom": bf(np.random.standard_normal((M, N)) * s),
         "v": bf((0.3 + 0.7 * np.random.standard_normal((M, R)) ** 2) / (t * t)),
         "w": bf(np.random.standard_normal((M, N)))}
    for name, x in (("a", a), ("b", b)):
        sc = (np.abs(x).reshape(R // BLK, BLK, N // BLK, BLK).max(axis=(1, 3)) / 448.0).astype(np.float32)
        d[name + "_bytes"] = e4m3fn_bytes(x / np.repeat(np.repeat(f64(sc), BLK, axis=0), BLK, axis=1))
        d[name + "_scale"] = sc
    return d


def reference(mom, v, w, a_bytes, a_scale, b_bytes, b_scale):
    a = e4m3fn_values(a_bytes) * np.repeat(np.repeat(f64(a_scale), BLK, axis=0), BLK, axis=1)
    b = e4m3fn_values(b_bytes) * np.repeat(np.repeat(f64(b_scale), BLK, axis=0), BLK, axis=1)
    r = mxq(f64(mom), 1, "e4m3") @ mxq(a, 1, "e4m3").T
    h = r / np.sqrt(f64(v))
    u = mxq(h, 1, "e4m3") @ mxq(b, 0, "e4m3")
    return f64(w) * KEEP - u

@@ -1,0 +1,343 @@
+from contextlib import ExitStack
+
+import concourse.mybir as mybir
+from concourse.masks import make_identity
+
+M, N, R = 2048, 1536, 512
+KEEP = 0.9
+
+FLOPS = 2 * 2 * M * N * R
+
+F32 = mybir.dt.float32
+BF16 = mybir.dt.bfloat16
+U32 = mybir.dt.uint32
+U8 = mybir.dt.uint8
+FP8 = mybir.dt.float8_e4m3fn
+FP8X4 = mybir.dt.float8_e4m3fn_x4
+ALU = mybir.AluOpType
+ACT = mybir.ActivationFunctionType
+
+P = 128
+TILES = M // P
+GROUPS = N // 512
+ROWBLK = R // P
+NBLK = N // P
+CHUNKS = N // 512
+A_SCALE = ["VVVVVVVVSSSS", "VVVVVVVVSSSS", "VVVVVVVVSSSS", "VVVVVVVVSSSS"]
+A_OUT = ["SV", "SV", "SV", "SV"]
+B_WIDEN = "VSS"
+B_OUT = ["VVSS", "VVSS", "VVSS"]
+B_AT = {1: 1, 3: 2}
+FIN = [0, 0, 1, 1, 1, 2, 3, 3, 4, 4, 4, 4, 4, 4, 4, 4, 5]
+
+
+def tile_lowrank_adam_style_step_d7_kernel(
+    tc, mom, v, w, a_bytes, a_scale, b_bytes, b_scale, out
+):
+    nc = tc.nc
+    mom_v = mom.rearrange("(p i) k -> p i k", i=TILES)
+    v_v = v.rearrange("(p i) r -> p i r", i=TILES)
+    w_v = w.rearrange("(p i) n -> p i n", i=TILES)
+    out_v = out.rearrange("(p i) n -> p i n", i=TILES)
+
+    with ExitStack() as ctx:
+        keep = ctx.enter_context(tc.tile_pool(name="keep", bufs=1))
+        momp = ctx.enter_context(tc.tile_pool(name="momp", bufs=10))
+        wp = ctx.enter_context(tc.tile_pool(name="wp", bufs=16))
+        widep = ctx.enter_context(tc.tile_pool(name="widep", bufs=4))
+        bp = ctx.enter_context(tc.tile_pool(name="bp", bufs=2))
+        work = ctx.enter_context(tc.tile_pool(name="work", bufs=2))
+        hp = ctx.enter_context(tc.tile_pool(name="hp", bufs=3))
+        hq_pool = ctx.enter_context(tc.tile_pool(name="hqp", bufs=8))
+        outp = ctx.enter_context(tc.tile_pool(name="outp", bufs=12))
+        ps_tr = ctx.enter_context(tc.psum_pool(name="ps_tr", bufs=3))
+        ps_r = ctx.enter_context(tc.psum_pool(name="ps_r", bufs=2))
+        ps_u = ctx.enter_context(tc.psum_pool(name="ps_u", bufs=3))
+
+        warm = keep.tile([P, 1], F32)
+        nc.vector.memset(warm[:], 1.0)
+        warm_o = keep.tile([P, 1], F32)
+        nc.scalar.activation(out=warm_o[:], in_=warm[:], func=ACT.Abs_reciprocal_sqrt)
+        ident = keep.tile([P, P], F32)
+        make_identity(nc, ident[:])
+        perm = keep.tile([P, P], F32)
+        nc.gpsimd.tensor_copy(
+            out=perm[:].rearrange("p (t m) -> p t m", t=4),
+            in_=ident[:].rearrange("p (m t) -> p t m", t=4),
+        )
+
+        as_all = keep.tile([P, ROWBLK * NBLK], F32)
+        nc.scalar.dma_start(
+            out=as_all[:], in_=a_scale.rearrange("i j -> (i j)").partition_broadcast(P)
+        )
+        bs_all = keep.tile([P, ROWBLK * NBLK], F32)
+        nc.scalar.dma_start(
+            out=bs_all[:], in_=b_scale.rearrange("i j -> (i j)").partition_broadcast(P)
+        )
+        a_b = [keep.tile([P, N], U8, name="a_b%d" % i) for i in range(ROWBLK)]
+        for i in range(ROWBLK):
+            nc.sync.dma_start(out=a_b[i][:], in_=a_bytes[P * i : P * (i + 1), :])
+        mom_t, v_t, w_t = {}, {}, {}
+        b_b = [keep.tile([P, 4, 512], U8, name="b_b%d" % c) for c in range(CHUNKS)]
+        b_rows = b_bytes.rearrange("(p t) n -> p t n", t=4)
+
+        def load_b(c):
+            nc.sync.dma_start(out=b_b[c][:], in_=b_rows[:, :, 512 * c : 512 * (c + 1)])
+
+        def load_mom(k):
+            mt = momp.tile([P, N], BF16, name="mom_t")
+            nc.sync.dma_start(out=mt[:], in_=mom_v[:, k, :])
+            mom_t[k] = mt
+
+        def load_v(j):
+            vt = keep.tile([P, 4, R], BF16, name="v_t%d" % j)
+            nc.sync.dma_start(out=vt[:], in_=v_v[:, 4 * j : 4 * j + 4, :])
+            v_t[j] = vt
+
+        def load_w(k):
+            wt = wp.tile([P, N], BF16, name="w_t")
+            nc.sync.dma_start(out=wt[:], in_=w_v[:, k, :])
+            w_t[k] = wt
+
+        load_mom(0)
+        load_mom(1)
+        load_b(0)
+        load_v(0)
+        load_mom(2)
+        load_mom(3)
+        load_b(1)
+        load_b(2)
+
+        b_sc = keep.tile([P, NBLK], F32)
+        for q in range(4):
+            rows = slice(32 * q, 32 * q + 32)
+            nc.gpsimd.tensor_copy(
+                out=b_sc[rows], in_=bs_all[rows, NBLK * q : NBLK * (q + 1)]
+            )
+
+        def cast(e, dst, src):
+            if e == "S":
+                nc.scalar.copy(out=dst, in_=src)
+            elif e == "G":
+                nc.gpsimd.tensor_copy(out=dst, in_=src)
+            else:
+                nc.vector.tensor_copy(out=dst, in_=src)
+
+        def scaled(e, dst, src, sc):
+            if e == "S":
+                nc.scalar.activation(out=dst, in_=src, func=ACT.Copy, scale=sc)
+            else:
+                nc.vector.tensor_scalar(out=dst, in0=src, scalar1=sc, scalar2=None, op0=ALU.mult)
+
+        a_g = keep.tile([P, GROUPS, 4 * R], BF16, align_bytes=64)
+        a_c = keep.tile([P, GROUPS, R], U32, align_bytes=64)
+        a_s = keep.tile([P, GROUPS, R], U8, align_bytes=64)
+        a_words = a_g[:].bitcast(F32).rearrange("p g (t m u) -> p g t m u", t=4, u=2)
+
+        def prepare_a(i):
+            wide = widep.tile([P, N], BF16, name="wide")
+            for j in range(NBLK):
+                cols = slice(P * j, P * (j + 1))
+                s = NBLK * i + j
+                scaled(A_SCALE[i][j], wide[:, cols], a_b[i][:, cols].bitcast(FP8), as_all[:, s : s + 1])
+            words = wide[:].bitcast(F32)
+            for b, (g0, g1) in enumerate(((0, 2), (2, 3))):
+                bank = ps_tr.tile([P, 4, P], F32, name="bank")
+                for g in range(g0, g1):
+                    for u in range(2):
+                        nc.tensor.transpose(
+                            bank[:, 2 * (g - g0) + u, :],
+                            words[:, 256 * g + u : 256 * (g + 1) : 2],
+                            perm[:],
+                        )
+                cast(
+                    A_OUT[i][b],
+                    a_words[:, g0:g1, :, 32 * i : 32 * i + 32, :],
+                    bank[:, 0 : 2 * (g1 - g0), :].rearrange("p (g u) (t m) -> p g t m u", u=2, t=4),
+                )
+
+        def quant_a(g):
+            nc.vector.quantize_mx(
+                out=a_c[:, g, :].bitcast(FP8X4), scales=a_s[:, g, :], in_=a_g[:, g, :]
+            )
+
+        st = {}
+
+        def transposes(k):
+            words = mom_t[k][:].bitcast(F32)
+            vwords = v_t[k // 4][:, k % 4, :].bitcast(F32)
+            bx = ps_tr.tile([P, 4, P], F32, name="bank")
+            for g in range(2):
+                for u in range(2):
+                    nc.tensor.transpose(
+                        bx[:, 2 * g + u, :], words[:, 256 * g + u : 256 * (g + 1) : 2], ident[:]
+                    )
+            by = ps_tr.tile([P, 4, P], F32, name="bank")
+            for u in range(2):
+                nc.tensor.transpose(by[:, u, :], words[:, 512 + u : 768 : 2], ident[:])
+            for u in range(2):
+                nc.tensor.transpose(by[:, 2 + u, :], vwords[:, u::2], ident[:])
+            if k % 2 == 0:
+                st[k] = {"mg": work.tile([P, 2 * GROUPS, 4 * P], BF16, align_bytes=64, name="mg")}
+            else:
+                st[k] = {"mg": st[k - 1]["mg"]}
+            mg_words = st[k]["mg"][:].bitcast(F32)
+            g0 = GROUPS * (k % 2)
+            nc.scalar.copy(
+                out=mg_words[:, g0 : g0 + 2, :].rearrange("p g (n u) -> p g n u", u=2),
+                in_=bx[:].rearrange("p (g u) n -> p g n u", u=2),
+            )
+            nc.scalar.copy(
+                out=mg_words[:, g0 + 2, :].rearrange("p (n u) -> p n u", u=2),
+                in_=by[:, 0:2, :].rearrange("p u n -> p n u"),
+            )
+            rs = hp.tile([P, P, 2, 2], F32, name="rs")
+            nc.scalar.activation(
+                out=rs[:],
+                in_=by[:, 2:4, :].bitcast(BF16).rearrange("p u (n e) -> p n u e", e=2),
+                func=ACT.Abs_reciprocal_sqrt,
+            )
+            st[k]["rs"] = rs
+
+        def quant_mom(k, part):
+            mg = st[k]["mg"]
+            if part == 0:
+                mc = work.tile([P, 2 * GROUPS, P], U32, align_bytes=64, name="mc")
+                ms = work.tile([P, 2 * GROUPS, P], U8, align_bytes=64, name="ms")
+                for kk in (k, k + 1):
+                    st[kk]["mc"], st[kk]["ms"] = mc, ms
+            mc, ms = st[k]["mc"], st[k]["ms"]
+            g0, g1 = ((0, 4), (4, 6))[part]
+            nc.vector.quantize_mx(
+                out=mc[:, g0:g1, :].rearrange("p g n -> p (g n)").bitcast(FP8X4),
+                scales=ms[:, g0:g1, :].rearrange("p g n -> p (g n)"),
+                in_=mg[:, g0:g1, :].rearrange("p g n -> p (g n)"),
+            )
+
+        def project(k):
+            mc, ms = st[k]["mc"], st[k]["ms"]
+            g0 = GROUPS * (k % 2)
+            r = ps_r.tile([P, 4, P], F32, name="r")
+            for t in range(4):
+                for g in range(GROUPS):
+                    nc.tensor.matmul_mx(
+                        out=r[:, t, :],
+                        lhsT=a_c[:, g, P * t : P * (t + 1)].bitcast(FP8X4),
+                        lhsT_scale=a_s[:, g, P * t : P * (t + 1)],
+                        rhs=mc[:, g0 + g, :].bitcast(FP8X4),
+                        rhs_scale=ms[:, g0 + g, :],
+                        start=(g == 0),
+                        stop=(g == GROUPS - 1),
+                    )
+            st[k]["r"] = r
+
+        def direction(k):
+            if k % 2 == 0:
+                st[k]["h"] = work.tile([P, 2, P, 4], BF16, align_bytes=64, name="h")
+            else:
+                st[k]["h"] = st[k - 1]["h"]
+            nc.vector.tensor_tensor(
+                out=st[k]["h"][:, k % 2],
+                in0=st[k]["r"][:].rearrange("p t n -> p n t"),
+                in1=st[k]["rs"][:].rearrange("p n u e -> p n (u e)"),
+                op=ALU.mult,
+            )
+
+        def quant_h(k):
+            hc = hq_pool.tile([P, 2 * P], U32, align_bytes=64, name="hc")
+            hs = hq_pool.tile([P, 2 * P], U8, align_bytes=64, name="hs")
+            nc.vector.quantize_mx(
+                out=hc[:].bitcast(FP8X4),
+                scales=hs[:],
+                in_=st[k]["h"][:].rearrange("p k n t -> p (k n t)"),
+            )
+            for kk in (k, k + 1):
+                st[kk]["hc"], st[kk]["hs"] = hc, hs
+
+        b_c = keep.tile([P, N], U32, align_bytes=64)
+        b_s = keep.tile([P, N], U8, align_bytes=64)
+
+        def prepare_b(c):
+            wide = bp.tile([P, 4, 512], BF16, name="b_wide")
+            cast(B_WIDEN[c], wide[:].rearrange("p t n -> p (t n)"), b_b[c][:].rearrange("p t n -> p (t n)").bitcast(FP8))
+            b_g = bp.tile([P, 512, 4], BF16, align_bytes=64, name="b_g")
+            for j in range(4):
+                cols = slice(P * j, P * (j + 1))
+                jj = 4 * c + j
+                scaled(
+                    B_OUT[c][j],
+                    b_g[:, cols, :],
+                    wide[:, :, cols].rearrange("p t n -> p n t"),
+                    b_sc[:, jj : jj + 1],
+                )
+            nc.vector.quantize_mx(
+                out=b_c[:, 512 * c : 512 * (c + 1)].bitcast(FP8X4),
+                scales=b_s[:, 512 * c : 512 * (c + 1)],
+                in_=b_g[:].rearrange("p n t -> p (n t)"),
+            )
+
+        def finish(k, c):
+            part = slice(P * (k % 2), P * (k % 2) + P)
+            cols = slice(512 * c, 512 * (c + 1))
+            u = ps_u.tile([P, 512], F32, name="u")
+            nc.tensor.matmul_mx(
+                out=u[:],
+                lhsT=st[k]["hc"][:, part].bitcast(FP8X4),
+                lhsT_scale=st[k]["hs"][:, part],
+                rhs=b_c[:, cols].bitcast(FP8X4),
+                rhs_scale=b_s[:, cols],
+                start=True,
+                stop=True,
+            )
+            o = outp.tile([P, 512], F32, name="o")
+            nc.vector.scalar_tensor_tensor(
+                out=o[:], in0=w_t[k][:, cols], scalar=KEEP, in1=u[:], op0=ALU.mult, op1=ALU.subtract
+            )
+            nc.sync.dma_start(out=out_v[:, k, cols], in_=o[:])
+
+        for i in range(ROWBLK):
+            prepare_a(i)
+        transposes(0)
+        transposes(1)
+        for g in range(GROUPS):
+            quant_a(g)
+        quant_mom(0, 0)
+        quant_mom(0, 1)
+        project(0)
+        project(1)
+        prepare_b(0)
+
+        todo = []
+        b_ready = [True, False, False]
+        for s in range(TILES + 1):
+            k = s
+            if k + 4 < TILES:
+                load_mom(k + 4)
+                if k % 4 == 0:
+                    load_v((k + 4) // 4)
+            if k < TILES:
+                load_w(k)
+            if k + 2 < TILES:
+                transposes(k + 2)
+            if k < TILES:
+                direction(k)
+            if k % 2 == 1 and k < TILES:
+                quant_h(k - 1)
+                todo += [(kk, c) for kk in (k - 1, k) for c in range(CHUNKS)]
+                if k + 2 < TILES:
+                    quant_mom(k + 1, 0)
+                    quant_mom(k + 1, 1)
+            if k % 2 == 1 and k + 2 < TILES:
+                project(k + 1)
+                project(k + 2)
+            n = 0
+            for x in list(todo):
+                if n < FIN[s] and b_ready[x[1]]:
+                    finish(*x)
+                    todo.remove(x)
+                    n += 1
+            if s in B_AT:
+                prepare_b(B_AT[s])
+                b_ready[B_AT[s]] = True
+        for x in todo:
+            finish(*x)

@@ -23,12 +23,7 @@ GROUPS = N // 512
 ROWBLK = R // P
 NBLK = N // P
 CHUNKS = N // 512
-A_SCALE = ["VVVVVVVVSSSS", "VVVVVVVVSSSS", "VVVVVVVVSSSS", "VVVVVVVVSSSS"]
-A_OUT = ["SV", "SV", "SV", "SV"]
-B_WIDEN = "VSS"
-B_OUT = ["VVSS", "VVSS", "VVSS"]
-B_AT = {1: 1, 3: 2}
-FIN = [0, 0, 1, 1, 1, 2, 3, 3, 4, 4, 4, 4, 4, 4, 4, 4, 5]
+A_BANKS = [("r", "r"), ("r", "r"), ("u", "u"), ("u", "u"), ("u", "u"), ("t", "bank"), ("r", "r"), ("r", "r")]
 
 
 def tile_lowrank_adam_style_step_d7_kernel(
@@ -39,55 +34,57 @@ def tile_lowrank_adam_style_step_d7_kernel(
     v_v = v.rearrange("(p i) r -> p i r", i=TILES)
     w_v = w.rearrange("(p i) n -> p i n", i=TILES)
     out_v = out.rearrange("(p i) n -> p i n", i=TILES)
+    a_rows = a_bytes.rearrange("(p t) k -> p t k", t=4)
+    b_rows = b_bytes.rearrange("(p t) n -> p t n", t=4)
 
     with ExitStack() as ctx:
         keep = ctx.enter_context(tc.tile_pool(name="keep", bufs=1))
-        momp = ctx.enter_context(tc.tile_pool(name="momp", bufs=10))
-        wp = ctx.enter_context(tc.tile_pool(name="wp", bufs=16))
-        widep = ctx.enter_context(tc.tile_pool(name="widep", bufs=4))
-        bp = ctx.enter_context(tc.tile_pool(name="bp", bufs=2))
-        work = ctx.enter_context(tc.tile_pool(name="work", bufs=2))
-        hp = ctx.enter_context(tc.tile_pool(name="hp", bufs=3))
-        hq_pool = ctx.enter_context(tc.tile_pool(name="hqp", bufs=8))
-        outp = ctx.enter_context(tc.tile_pool(name="outp", bufs=12))
+        momp = ctx.enter_context(tc.tile_pool(name="momp", bufs=6))
+        wp = ctx.enter_context(tc.tile_pool(name="wp", bufs=6))
+        widep = ctx.enter_context(tc.tile_pool(name="widep", bufs=6))
+        work = ctx.enter_context(tc.tile_pool(name="work", bufs=3))
+        rsp = ctx.enter_context(tc.tile_pool(name="rsp", bufs=5))
+        outp = ctx.enter_context(tc.tile_pool(name="outp", bufs=3))
         ps_tr = ctx.enter_context(tc.psum_pool(name="ps_tr", bufs=3))
         ps_r = ctx.enter_context(tc.psum_pool(name="ps_r", bufs=2))
         ps_u = ctx.enter_context(tc.psum_pool(name="ps_u", bufs=3))
+        ctx.enter_context(tc.manual_schedule())
 
         warm = keep.tile([P, 1], F32)
         nc.vector.memset(warm[:], 1.0)
         warm_o = keep.tile([P, 1], F32)
+        a_sc = keep.tile([P, NBLK], F32)
+        b_sc = keep.tile([P, NBLK], F32)
+        a_all = keep.tile([P, ROWBLK * NBLK], F32)
+        b_all = keep.tile([P, ROWBLK * NBLK], F32)
+        nc.scalar.dma_start(out=a_all[:], in_=a_scale.rearrange("i j -> (i j)").partition_broadcast(P))
+        nc.scalar.dma_start(out=b_all[:], in_=b_scale.rearrange("i j -> (i j)").partition_broadcast(P))
+        for q in range(4):
+            rows = slice(32 * q, 32 * q + 32)
+            nc.vector.tensor_copy(out=a_sc[rows], in_=a_all[rows, NBLK * q : NBLK * (q + 1)])
         nc.scalar.activation(out=warm_o[:], in_=warm[:], func=ACT.Abs_reciprocal_sqrt)
         ident = keep.tile([P, P], F32)
         make_identity(nc, ident[:])
-        perm = keep.tile([P, P], F32)
-        nc.gpsimd.tensor_copy(
-            out=perm[:].rearrange("p (t m) -> p t m", t=4),
-            in_=ident[:].rearrange("p (m t) -> p t m", t=4),
-        )
+        for q in range(4):
+            rows = slice(32 * q, 32 * q + 32)
+            nc.gpsimd.tensor_copy(out=b_sc[rows], in_=b_all[rows, NBLK * q : NBLK * (q + 1)])
 
-        as_all = keep.tile([P, ROWBLK * NBLK], F32)
-        nc.scalar.dma_start(
-            out=as_all[:], in_=a_scale.rearrange("i j -> (i j)").partition_broadcast(P)
-        )
-        bs_all = keep.tile([P, ROWBLK * NBLK], F32)
-        nc.scalar.dma_start(
-            out=bs_all[:], in_=b_scale.rearrange("i j -> (i j)").partition_broadcast(P)
-        )
-        a_b = [keep.tile([P, N], U8, name="a_b%d" % i) for i in range(ROWBLK)]
-        for i in range(ROWBLK):
-            nc.sync.dma_start(out=a_b[i][:], in_=a_bytes[P * i : P * (i + 1), :])
-        mom_t, v_t, w_t = {}, {}, {}
-        b_b = [keep.tile([P, 4, 512], U8, name="b_b%d" % c) for c in range(CHUNKS)]
-        b_rows = b_bytes.rearrange("(p t) n -> p t n", t=4)
+        mom_t, v_t, w_t, o_t = {}, {}, {}, {}
+        a_b = keep.tile([P, 4, N], U8)
+        b_b = keep.tile([P, 4, N], U8)
 
-        def load_b(c):
-            nc.sync.dma_start(out=b_b[c][:], in_=b_rows[:, :, 512 * c : 512 * (c + 1)])
+        def load_a(t):
+            nc.sync.dma_start(out=a_b[:, t, :], in_=a_rows[:, t, :])
 
-        def load_mom(k):
-            mt = momp.tile([P, N], BF16, name="mom_t")
-            nc.sync.dma_start(out=mt[:], in_=mom_v[:, k, :])
-            mom_t[k] = mt
+        def load_b(h):
+            nc.sync.dma_start(out=b_b[:, 2 * h : 2 * h + 2, :], in_=b_rows[:, 2 * h : 2 * h + 2, :])
+
+        def load_mom(k, n=2):
+            if k % 2 == 0:
+                mom_t[k] = momp.tile([P, 2, N], BF16, name="mom_t")
+                mom_t[k + 1] = mom_t[k]
+            h = k % 2
+            nc.sync.dma_start(out=mom_t[k][:, h : h + n, :], in_=mom_v[:, k : k + n, :])
 
         def load_v(j):
             vt = keep.tile([P, 4, R], BF16, name="v_t%d" % j)
@@ -95,31 +92,13 @@ def tile_lowrank_adam_style_step_d7_kernel(
             v_t[j] = vt
 
         def load_w(k):
-            wt = wp.tile([P, N], BF16, name="w_t")
-            nc.sync.dma_start(out=wt[:], in_=w_v[:, k, :])
-            w_t[k] = wt
-
-        load_mom(0)
-        load_mom(1)
-        load_b(0)
-        load_v(0)
-        load_mom(2)
-        load_mom(3)
-        load_b(1)
-        load_b(2)
-
-        b_sc = keep.tile([P, NBLK], F32)
-        for q in range(4):
-            rows = slice(32 * q, 32 * q + 32)
-            nc.gpsimd.tensor_copy(
-                out=b_sc[rows], in_=bs_all[rows, NBLK * q : NBLK * (q + 1)]
-            )
+            wt = wp.tile([P, 2, N], BF16, name="w_t")
+            nc.sync.dma_start(out=wt[:], in_=w_v[:, k : k + 2, :])
+            w_t[k] = w_t[k + 1] = wt
 
         def cast(e, dst, src):
             if e == "S":
                 nc.scalar.copy(out=dst, in_=src)
-            elif e == "G":
-                nc.gpsimd.tensor_copy(out=dst, in_=src)
             else:
                 nc.vector.tensor_copy(out=dst, in_=src)
 
@@ -132,39 +111,69 @@ def tile_lowrank_adam_style_step_d7_kernel(
         a_g = keep.tile([P, GROUPS, 4 * R], BF16, align_bytes=64)
         a_c = keep.tile([P, GROUPS, R], U32, align_bytes=64)
         a_s = keep.tile([P, GROUPS, R], U8, align_bytes=64)
-        a_words = a_g[:].bitcast(F32).rearrange("p g (t m u) -> p g t m u", t=4, u=2)
+        a_words = a_g[:].bitcast(F32).rearrange("p g (m u) -> p g m u", u=2)
+        a_wide, a_bank = {}, {}
 
-        def prepare_a(i):
-            wide = widep.tile([P, N], BF16, name="wide")
-            for j in range(NBLK):
+        def scale_a(t, js, e):
+            if t not in a_wide:
+                a_wide[t] = widep.tile([P, N], BF16, name="wide")
+            for j in js:
                 cols = slice(P * j, P * (j + 1))
-                s = NBLK * i + j
-                scaled(A_SCALE[i][j], wide[:, cols], a_b[i][:, cols].bitcast(FP8), as_all[:, s : s + 1])
-            words = wide[:].bitcast(F32)
-            for b, (g0, g1) in enumerate(((0, 2), (2, 3))):
-                bank = ps_tr.tile([P, 4, P], F32, name="bank")
+                scaled(e, a_wide[t][:, cols], a_b[:, t, cols].bitcast(FP8), a_sc[:, j : j + 1])
+
+        def turn_a(t, bs=(0, 1)):
+            words = a_wide[t][:].bitcast(F32)
+            for b in bs:
+                g0, g1 = ((0, 2), (2, 3))[b]
+                pool, name = A_BANKS[2 * t + b]
+                bank = {"t": ps_tr, "r": ps_r, "u": ps_u}[pool].tile([P, 4, P], F32, name=name)
+                a_bank[t, b] = bank
                 for g in range(g0, g1):
                     for u in range(2):
                         nc.tensor.transpose(
                             bank[:, 2 * (g - g0) + u, :],
                             words[:, 256 * g + u : 256 * (g + 1) : 2],
-                            perm[:],
+                            ident[:],
                         )
-                cast(
-                    A_OUT[i][b],
-                    a_words[:, g0:g1, :, 32 * i : 32 * i + 32, :],
-                    bank[:, 0 : 2 * (g1 - g0), :].rearrange("p (g u) (t m) -> p g t m u", u=2, t=4),
-                )
+
+        def empty_a(t, b, e):
+            g0, g1 = ((0, 2), (2, 3))[b]
+            cast(
+                e,
+                a_words[:, g0:g1, P * t : P * (t + 1), :],
+                a_bank[t, b][:, 0 : 2 * (g1 - g0), :].rearrange("p (g u) m -> p g m u", u=2),
+            )
 
         def quant_a(g):
             nc.vector.quantize_mx(
                 out=a_c[:, g, :].bitcast(FP8X4), scales=a_s[:, g, :], in_=a_g[:, g, :]
             )
 
-        st = {}
+        b_wide = keep.tile([P, 4, N], BF16)
+        b_g = keep.tile([P, N, 4], BF16, align_bytes=64)
+        b_c = keep.tile([P, N], U32, align_bytes=64)
+        b_s = keep.tile([P, N], U8, align_bytes=64)
 
-        def transposes(k):
-            words = mom_t[k][:].bitcast(F32)
+        def widen_b(t, e):
+            cast(e, b_wide[:, t, :], b_b[:, t, :].bitcast(FP8))
+
+        def scale_b(js, e):
+            for j in js:
+                cols = slice(P * j, P * (j + 1))
+                scaled(e, b_g[:, cols, :], b_wide[:, :, cols].rearrange("p t n -> p n t"), b_sc[:, j : j + 1])
+
+        def quant_b(c):
+            cols = slice(512 * c, 512 * (c + 1))
+            nc.vector.quantize_mx(
+                out=b_c[:, cols].bitcast(FP8X4),
+                scales=b_s[:, cols],
+                in_=b_g[:, cols, :].rearrange("p n t -> p (n t)"),
+            )
+
+        st = {k: {} for k in range(TILES)}
+
+        def turn(k):
+            words = mom_t[k][:, k % 2, :].bitcast(F32)
             vwords = v_t[k // 4][:, k % 4, :].bitcast(F32)
             bx = ps_tr.tile([P, 4, P], F32, name="bank")
             for g in range(2):
@@ -177,46 +186,42 @@ def tile_lowrank_adam_style_step_d7_kernel(
                 nc.tensor.transpose(by[:, u, :], words[:, 512 + u : 768 : 2], ident[:])
             for u in range(2):
                 nc.tensor.transpose(by[:, 2 + u, :], vwords[:, u::2], ident[:])
-            if k % 2 == 0:
-                st[k] = {"mg": work.tile([P, 2 * GROUPS, 4 * P], BF16, align_bytes=64, name="mg")}
-            else:
-                st[k] = {"mg": st[k - 1]["mg"]}
-            mg_words = st[k]["mg"][:].bitcast(F32)
-            g0 = GROUPS * (k % 2)
+            st[k]["bx"], st[k]["by"] = bx, by
+
+        def empty(k):
+            bx, by = st[k]["bx"], st[k]["by"]
+            mg = work.tile([P, GROUPS, 4 * P], BF16, align_bytes=64, name="mg")
+            mg_words = mg[:].bitcast(F32)
             nc.scalar.copy(
-                out=mg_words[:, g0 : g0 + 2, :].rearrange("p g (n u) -> p g n u", u=2),
+                out=mg_words[:, 0:2, :].rearrange("p g (n u) -> p g n u", u=2),
                 in_=bx[:].rearrange("p (g u) n -> p g n u", u=2),
             )
             nc.scalar.copy(
-                out=mg_words[:, g0 + 2, :].rearrange("p (n u) -> p n u", u=2),
+                out=mg_words[:, 2, :].rearrange("p (n u) -> p n u", u=2),
                 in_=by[:, 0:2, :].rearrange("p u n -> p n u"),
             )
-            rs = hp.tile([P, P, 2, 2], F32, name="rs")
+            rs = rsp.tile([P, P, 2, 2], F32, name="rs")
             nc.scalar.activation(
                 out=rs[:],
                 in_=by[:, 2:4, :].bitcast(BF16).rearrange("p u (n e) -> p n u e", e=2),
                 func=ACT.Abs_reciprocal_sqrt,
             )
-            st[k]["rs"] = rs
+            st[k]["mg"], st[k]["rs"] = mg, rs
 
-        def quant_mom(k, part):
+        def quant_mom(k):
             mg = st[k]["mg"]
-            if part == 0:
-                mc = work.tile([P, 2 * GROUPS, P], U32, align_bytes=64, name="mc")
-                ms = work.tile([P, 2 * GROUPS, P], U8, align_bytes=64, name="ms")
-                for kk in (k, k + 1):
-                    st[kk]["mc"], st[kk]["ms"] = mc, ms
-            mc, ms = st[k]["mc"], st[k]["ms"]
-            g0, g1 = ((0, 4), (4, 6))[part]
-            nc.vector.quantize_mx(
-                out=mc[:, g0:g1, :].rearrange("p g n -> p (g n)").bitcast(FP8X4),
-                scales=ms[:, g0:g1, :].rearrange("p g n -> p (g n)"),
-                in_=mg[:, g0:g1, :].rearrange("p g n -> p (g n)"),
-            )
+            mc = work.tile([P, GROUPS, P], U32, align_bytes=64, name="mc")
+            ms = work.tile([P, GROUPS, P], U8, align_bytes=64, name="ms")
+            for g0, g1 in ((0, 2), (2, 3)):
+                nc.vector.quantize_mx(
+                    out=mc[:, g0:g1, :].rearrange("p g n -> p (g n)").bitcast(FP8X4),
+                    scales=ms[:, g0:g1, :].rearrange("p g n -> p (g n)"),
+                    in_=mg[:, g0:g1, :].rearrange("p g n -> p (g n)"),
+                )
+            st[k]["mc"], st[k]["ms"] = mc, ms
 
         def project(k):
             mc, ms = st[k]["mc"], st[k]["ms"]
-            g0 = GROUPS * (k % 2)
             r = ps_r.tile([P, 4, P], F32, name="r")
             for t in range(4):
                 for g in range(GROUPS):
@@ -224,120 +229,162 @@ def tile_lowrank_adam_style_step_d7_kernel(
                         out=r[:, t, :],
                         lhsT=a_c[:, g, P * t : P * (t + 1)].bitcast(FP8X4),
                         lhsT_scale=a_s[:, g, P * t : P * (t + 1)],
-                        rhs=mc[:, g0 + g, :].bitcast(FP8X4),
-                        rhs_scale=ms[:, g0 + g, :],
+                        rhs=mc[:, g, :].bitcast(FP8X4),
+                        rhs_scale=ms[:, g, :],
                         start=(g == 0),
                         stop=(g == GROUPS - 1),
                     )
             st[k]["r"] = r
 
         def direction(k):
-            if k % 2 == 0:
-                st[k]["h"] = work.tile([P, 2, P, 4], BF16, align_bytes=64, name="h")
-            else:
-                st[k]["h"] = st[k - 1]["h"]
+            h = work.tile([P, P, 4], BF16, align_bytes=64, name="h")
             nc.vector.tensor_tensor(
-                out=st[k]["h"][:, k % 2],
+                out=h[:],
                 in0=st[k]["r"][:].rearrange("p t n -> p n t"),
                 in1=st[k]["rs"][:].rearrange("p n u e -> p n (u e)"),
                 op=ALU.mult,
             )
+            st[k]["h"] = h
 
         def quant_h(k):
-            hc = hq_pool.tile([P, 2 * P], U32, align_bytes=64, name="hc")
-            hs = hq_pool.tile([P, 2 * P], U8, align_bytes=64, name="hs")
+            hc = work.tile([P, P], U32, align_bytes=64, name="hc")
+            hs = work.tile([P, P], U8, align_bytes=64, name="hs")
             nc.vector.quantize_mx(
                 out=hc[:].bitcast(FP8X4),
                 scales=hs[:],
-                in_=st[k]["h"][:].rearrange("p k n t -> p (k n t)"),
+                in_=st[k]["h"][:].rearrange("p n t -> p (n t)"),
             )
-            for kk in (k, k + 1):
-                st[kk]["hc"], st[kk]["hs"] = hc, hs
+            st[k]["hc"], st[k]["hs"] = hc, hs
 
-        b_c = keep.tile([P, N], U32, align_bytes=64)
-        b_s = keep.tile([P, N], U8, align_bytes=64)
-
-        def prepare_b(c):
-            wide = bp.tile([P, 4, 512], BF16, name="b_wide")
-            cast(B_WIDEN[c], wide[:].rearrange("p t n -> p (t n)"), b_b[c][:].rearrange("p t n -> p (t n)").bitcast(FP8))
-            b_g = bp.tile([P, 512, 4], BF16, align_bytes=64, name="b_g")
-            for j in range(4):
-                cols = slice(P * j, P * (j + 1))
-                jj = 4 * c + j
-                scaled(
-                    B_OUT[c][j],
-                    b_g[:, cols, :],
-                    wide[:, :, cols].rearrange("p t n -> p n t"),
-                    b_sc[:, jj : jj + 1],
+        def lift(k):
+            st[k]["u"] = []
+            for c in range(CHUNKS):
+                cols = slice(512 * c, 512 * (c + 1))
+                u = ps_u.tile([P, 4, P], F32, name="u")
+                nc.tensor.matmul_mx(
+                    out=u[:].rearrange("p a b -> p (a b)"),
+                    lhsT=st[k]["hc"][:].bitcast(FP8X4),
+                    lhsT_scale=st[k]["hs"][:],
+                    rhs=b_c[:, cols].bitcast(FP8X4),
+                    rhs_scale=b_s[:, cols],
+                    start=True,
+                    stop=True,
                 )
-            nc.vector.quantize_mx(
-                out=b_c[:, 512 * c : 512 * (c + 1)].bitcast(FP8X4),
-                scales=b_s[:, 512 * c : 512 * (c + 1)],
-                in_=b_g[:].rearrange("p n t -> p (n t)"),
-            )
+                st[k]["u"].append(u)
 
-        def finish(k, c):
-            part = slice(P * (k % 2), P * (k % 2) + P)
-            cols = slice(512 * c, 512 * (c + 1))
-            u = ps_u.tile([P, 512], F32, name="u")
-            nc.tensor.matmul_mx(
-                out=u[:],
-                lhsT=st[k]["hc"][:, part].bitcast(FP8X4),
-                lhsT_scale=st[k]["hs"][:, part],
-                rhs=b_c[:, cols].bitcast(FP8X4),
-                rhs_scale=b_s[:, cols],
-                start=True,
-                stop=True,
-            )
-            o = outp.tile([P, 512], F32, name="o")
-            nc.vector.scalar_tensor_tensor(
-                out=o[:], in0=w_t[k][:, cols], scalar=KEEP, in1=u[:], op0=ALU.mult, op1=ALU.subtract
-            )
-            nc.sync.dma_start(out=out_v[:, k, cols], in_=o[:])
+        def finish(k):
+            if k % 2 == 0:
+                o_t[k] = o_t[k + 1] = outp.tile([P, 2, N], F32, name="o")
+            for c in range(CHUNKS):
+                cols = slice(512 * c, 512 * (c + 1))
+                nc.vector.scalar_tensor_tensor(
+                    out=o_t[k][:, k % 2, cols],
+                    in0=w_t[k][:, k % 2, cols],
+                    scalar=KEEP,
+                    in1=st[k]["u"][c][:].rearrange("p a b -> p (a b)"),
+                    op0=ALU.mult,
+                    op1=ALU.subtract,
+                )
+                if k == TILES - 1:
+                    nc.sync.dma_start(out=out_v[:, k, cols], in_=o_t[k][:, 1, cols])
+            if k == TILES - 2:
+                nc.sync.dma_start(out=out_v[:, k, :], in_=o_t[k][:, 0, :])
+            elif k % 2 == 1 and k < TILES - 1:
+                nc.sync.dma_start(out=out_v[:, k - 1 : k + 1, :], in_=o_t[k][:])
 
-        for i in range(ROWBLK):
-            prepare_a(i)
-        transposes(0)
-        transposes(1)
-        for g in range(GROUPS):
-            quant_a(g)
-        quant_mom(0, 0)
-        quant_mom(0, 1)
+        for t in range(4):
+            load_a(t)
+        load_mom(0, 1)
+        load_v(0)
+        load_mom(1, 1)
+        load_b(0)
+        load_b(1)
+        load_mom(2)
+        load_w(0)
+        load_v(1)
+        load_mom(4)
+        load_w(2)
+        load_mom(6)
+        load_w(4)
+        load_v(2)
+        load_mom(8)
+        load_w(6)
+
+        V_J, S_J = range(0, 8), range(8, 12)
+        scale_a(0, V_J, "V")
+        scale_a(0, S_J, "S")
+        turn_a(0)
+        scale_a(1, V_J, "V")
+        scale_a(1, S_J, "S")
+        turn_a(1)
+        scale_a(2, V_J, "V")
+        empty_a(0, 0, "S")
+        scale_a(2, S_J, "S")
+        turn_a(2)
+        empty_a(0, 1, "V")
+        scale_a(3, V_J, "V")
+        empty_a(1, 0, "S")
+        scale_a(3, S_J, "S")
+        turn_a(3)
+        turn(0)
+        empty_a(1, 1, "V")
+        empty_a(2, 1, "V")
+        empty_a(2, 0, "S")
+        empty_a(3, 0, "V")
+        empty_a(3, 1, "V")
+        empty(0)
+        turn(1)
+        empty(1)
+        quant_a(0)
+        quant_a(1)
+        quant_a(2)
+        quant_mom(0)
         project(0)
+        turn(2)
+        widen_b(0, "S")
+        widen_b(1, "V")
+        widen_b(2, "V")
+        quant_mom(1)
         project(1)
-        prepare_b(0)
-
-        todo = []
-        b_ready = [True, False, False]
-        for s in range(TILES + 1):
-            k = s
-            if k + 4 < TILES:
-                load_mom(k + 4)
-                if k % 4 == 0:
-                    load_v((k + 4) // 4)
-            if k < TILES:
-                load_w(k)
-            if k + 2 < TILES:
-                transposes(k + 2)
-            if k < TILES:
-                direction(k)
-            if k % 2 == 1 and k < TILES:
-                quant_h(k - 1)
-                todo += [(kk, c) for kk in (k - 1, k) for c in range(CHUNKS)]
-                if k + 2 < TILES:
-                    quant_mom(k + 1, 0)
-                    quant_mom(k + 1, 1)
-            if k % 2 == 1 and k + 2 < TILES:
-                project(k + 1)
-                project(k + 2)
-            n = 0
-            for x in list(todo):
-                if n < FIN[s] and b_ready[x[1]]:
-                    finish(*x)
-                    todo.remove(x)
-                    n += 1
-            if s in B_AT:
-                prepare_b(B_AT[s])
-                b_ready[B_AT[s]] = True
-        for x in todo:
-            finish(*x)
+        widen_b(3, "V")
+        empty(2)
+        scale_b(range(0, 4), "V")
+        direction(0)
+        scale_b(range(8, 10), "S")
+        quant_mom(2)
+        quant_h(0)
+        turn(3)
+        scale_b(range(4, 8), "V")
+        scale_b(range(10, 12), "S")
+        empty(3)
+        direction(1)
+        quant_b(0)
+        quant_h(1)
+        quant_b(1)
+        quant_b(2)
+        lift(0)
+        project(2)
+        quant_mom(3)
+        for s in range(2, TILES + 2):
+            if s + 2 < TILES:
+                turn(s + 2)
+            finish(s - 2)
+            if s % 2 == 1:
+                if s + 7 < TILES:
+                    load_mom(s + 7)
+                if s + 5 < TILES:
+                    load_w(s + 5)
+                if s == 3:
+                    load_v(3)
+            if s + 2 < TILES:
+                empty(s + 2)
+            if s < TILES:
+                direction(s)
+            if s + 1 < TILES:
+                project(s + 1)
+            if s - 1 < TILES:
+                lift(s - 1)
+            if s + 2 < TILES:
+                quant_mom(s + 2)
+            if s < TILES:
+                quant_h(s)

@@ -40,11 +40,14 @@ def tile_lowrank_adam_style_step_d7_kernel(
     with ExitStack() as ctx:
         keep = ctx.enter_context(tc.tile_pool(name="keep", bufs=1))
         momp = ctx.enter_context(tc.tile_pool(name="momp", bufs=6))
-        wp = ctx.enter_context(tc.tile_pool(name="wp", bufs=6))
-        widep = ctx.enter_context(tc.tile_pool(name="widep", bufs=6))
+        wp = ctx.enter_context(tc.tile_pool(name="wp", bufs=8))
+        widep = ctx.enter_context(tc.tile_pool(name="widep", bufs=4))
+        bp = ctx.enter_context(tc.tile_pool(name="bp", bufs=2))
+        hqp = ctx.enter_context(tc.tile_pool(name="hqp", bufs=8))
         work = ctx.enter_context(tc.tile_pool(name="work", bufs=3))
+        shp = ctx.enter_context(tc.tile_pool(name="shp", bufs=2))
         rsp = ctx.enter_context(tc.tile_pool(name="rsp", bufs=5))
-        outp = ctx.enter_context(tc.tile_pool(name="outp", bufs=3))
+        outp = ctx.enter_context(tc.tile_pool(name="outp", bufs=14))
         ps_tr = ctx.enter_context(tc.psum_pool(name="ps_tr", bufs=3))
         ps_r = ctx.enter_context(tc.psum_pool(name="ps_r", bufs=2))
         ps_u = ctx.enter_context(tc.psum_pool(name="ps_u", bufs=3))
@@ -71,13 +74,13 @@ def tile_lowrank_adam_style_step_d7_kernel(
 
         mom_t, v_t, w_t, o_t = {}, {}, {}, {}
         a_b = keep.tile([P, 4, N], U8)
-        b_b = keep.tile([P, 4, N], U8)
+        b_b = [keep.tile([P, 4, 512], U8, name="b_b%d" % c) for c in range(CHUNKS)]
 
         def load_a(t):
             nc.sync.dma_start(out=a_b[:, t, :], in_=a_rows[:, t, :])
 
-        def load_b(h):
-            nc.sync.dma_start(out=b_b[:, 2 * h : 2 * h + 2, :], in_=b_rows[:, 2 * h : 2 * h + 2, :])
+        def load_b(c):
+            nc.sync.dma_start(out=b_b[c][:], in_=b_rows[:, :, 512 * c : 512 * (c + 1)])
 
         def load_mom(k, n=2):
             if k % 2 == 0:
@@ -149,28 +152,44 @@ def tile_lowrank_adam_style_step_d7_kernel(
                 out=a_c[:, g, :].bitcast(FP8X4), scales=a_s[:, g, :], in_=a_g[:, g, :]
             )
 
-        b_wide = keep.tile([P, 4, N], BF16)
-        b_g = keep.tile([P, N, 4], BF16, align_bytes=64)
         b_c = keep.tile([P, N], U32, align_bytes=64)
         b_s = keep.tile([P, N], U8, align_bytes=64)
+        b_wide, b_g = {}, {}
 
-        def widen_b(t, e):
-            cast(e, b_wide[:, t, :], b_b[:, t, :].bitcast(FP8))
+        def widen_b(c, t0, t1, e):
+            if c not in b_wide:
+                b_wide[c] = bp.tile([P, 4, 512], BF16, name="b_wide")
+            cast(
+                e,
+                b_wide[c][:, t0:t1, :].rearrange("p t n -> p (t n)"),
+                b_b[c][:, t0:t1, :].rearrange("p t n -> p (t n)").bitcast(FP8),
+            )
 
-        def scale_b(js, e):
+        def scale_b(c, js, e):
+            if c not in b_g:
+                b_g[c] = bp.tile([P, 512, 4], BF16, align_bytes=64, name="b_g")
             for j in js:
                 cols = slice(P * j, P * (j + 1))
-                scaled(e, b_g[:, cols, :], b_wide[:, :, cols].rearrange("p t n -> p n t"), b_sc[:, j : j + 1])
+                jj = 4 * c + j
+                scaled(e, b_g[c][:, cols, :], b_wide[c][:, :, cols].rearrange("p t n -> p n t"), b_sc[:, jj : jj + 1])
 
         def quant_b(c):
             cols = slice(512 * c, 512 * (c + 1))
             nc.vector.quantize_mx(
                 out=b_c[:, cols].bitcast(FP8X4),
                 scales=b_s[:, cols],
-                in_=b_g[:, cols, :].rearrange("p n t -> p (n t)"),
+                in_=b_g[c][:].rearrange("p n t -> p (n t)"),
             )
 
         st = {k: {} for k in range(TILES)}
+
+        def shuffle(k):
+            words = mom_t[k][:, k % 2, :].bitcast(F32)
+            vwords = v_t[k // 4][:, k % 4, :].bitcast(F32)
+            sh = shp.tile([P, 4, P], F32, name="sh")
+            nc.scalar.copy(out=sh[:, 0:2, :], in_=words[:, 512:768].rearrange("p (n u) -> p u n", u=2))
+            nc.scalar.copy(out=sh[:, 2:4, :], in_=vwords.rearrange("p (n u) -> p u n", u=2))
+            st[k]["sh"] = sh
 
         def turn(k):
             words = mom_t[k][:, k % 2, :].bitcast(F32)
@@ -183,9 +202,13 @@ def tile_lowrank_adam_style_step_d7_kernel(
                     )
             by = ps_tr.tile([P, 4, P], F32, name="bank")
             for u in range(2):
-                nc.tensor.transpose(by[:, u, :], words[:, 512 + u : 768 : 2], ident[:])
+                nc.tensor.transpose(
+                    by[:, u, :], st[k]["sh"][:, u, :] if "sh" in st[k] else words[:, 512 + u : 768 : 2], ident[:]
+                )
             for u in range(2):
-                nc.tensor.transpose(by[:, 2 + u, :], vwords[:, u::2], ident[:])
+                nc.tensor.transpose(
+                    by[:, 2 + u, :], st[k]["sh"][:, 2 + u, :] if "sh" in st[k] else vwords[:, u::2], ident[:]
+                )
             st[k]["bx"], st[k]["by"] = bx, by
 
         def empty(k):
@@ -208,33 +231,33 @@ def tile_lowrank_adam_style_step_d7_kernel(
             )
             st[k]["mg"], st[k]["rs"] = mg, rs
 
-        def quant_mom(k):
+        def quant_mom(k, parts=(0, 1)):
             mg = st[k]["mg"]
-            mc = work.tile([P, GROUPS, P], U32, align_bytes=64, name="mc")
-            ms = work.tile([P, GROUPS, P], U8, align_bytes=64, name="ms")
-            for g0, g1 in ((0, 2), (2, 3)):
+            if 0 in parts:
+                st[k]["mc"] = work.tile([P, GROUPS, P], U32, align_bytes=64, name="mc")
+                st[k]["ms"] = work.tile([P, GROUPS, P], U8, align_bytes=64, name="ms")
+            mc, ms = st[k]["mc"], st[k]["ms"]
+            for g0, g1 in [((0, 2), (2, 3))[x] for x in parts]:
                 nc.vector.quantize_mx(
                     out=mc[:, g0:g1, :].rearrange("p g n -> p (g n)").bitcast(FP8X4),
                     scales=ms[:, g0:g1, :].rearrange("p g n -> p (g n)"),
                     in_=mg[:, g0:g1, :].rearrange("p g n -> p (g n)"),
                 )
-            st[k]["mc"], st[k]["ms"] = mc, ms
 
-        def project(k):
+        def project(k, t):
             mc, ms = st[k]["mc"], st[k]["ms"]
-            r = ps_r.tile([P, 4, P], F32, name="r")
-            for t in range(4):
-                for g in range(GROUPS):
-                    nc.tensor.matmul_mx(
-                        out=r[:, t, :],
-                        lhsT=a_c[:, g, P * t : P * (t + 1)].bitcast(FP8X4),
-                        lhsT_scale=a_s[:, g, P * t : P * (t + 1)],
-                        rhs=mc[:, g, :].bitcast(FP8X4),
-                        rhs_scale=ms[:, g, :],
-                        start=(g == 0),
-                        stop=(g == GROUPS - 1),
-                    )
-            st[k]["r"] = r
+            if t == 0:
+                st[k]["r"] = ps_r.tile([P, 4, P], F32, name="r")
+            for g in range(GROUPS):
+                nc.tensor.matmul_mx(
+                    out=st[k]["r"][:, t, :],
+                    lhsT=a_c[:, g, P * t : P * (t + 1)].bitcast(FP8X4),
+                    lhsT_scale=a_s[:, g, P * t : P * (t + 1)],
+                    rhs=mc[:, g, :].bitcast(FP8X4),
+                    rhs_scale=ms[:, g, :],
+                    start=(g == 0),
+                    stop=(g == GROUPS - 1),
+                )
 
         def direction(k):
             h = work.tile([P, P, 4], BF16, align_bytes=64, name="h")
@@ -247,8 +270,8 @@ def tile_lowrank_adam_style_step_d7_kernel(
             st[k]["h"] = h
 
         def quant_h(k):
-            hc = work.tile([P, P], U32, align_bytes=64, name="hc")
-            hs = work.tile([P, P], U8, align_bytes=64, name="hs")
+            hc = hqp.tile([P, P], U32, align_bytes=64, name="hc")
+            hs = hqp.tile([P, P], U8, align_bytes=64, name="hs")
             nc.vector.quantize_mx(
                 out=hc[:].bitcast(FP8X4),
                 scales=hs[:],
@@ -256,59 +279,53 @@ def tile_lowrank_adam_style_step_d7_kernel(
             )
             st[k]["hc"], st[k]["hs"] = hc, hs
 
-        def lift(k):
-            st[k]["u"] = []
-            for c in range(CHUNKS):
-                cols = slice(512 * c, 512 * (c + 1))
-                u = ps_u.tile([P, 4, P], F32, name="u")
-                nc.tensor.matmul_mx(
-                    out=u[:].rearrange("p a b -> p (a b)"),
-                    lhsT=st[k]["hc"][:].bitcast(FP8X4),
-                    lhsT_scale=st[k]["hs"][:],
-                    rhs=b_c[:, cols].bitcast(FP8X4),
-                    rhs_scale=b_s[:, cols],
-                    start=True,
-                    stop=True,
-                )
-                st[k]["u"].append(u)
+        u_bank = {}
 
-        def finish(k):
-            if k % 2 == 0:
-                o_t[k] = o_t[k + 1] = outp.tile([P, 2, N], F32, name="o")
-            for c in range(CHUNKS):
-                cols = slice(512 * c, 512 * (c + 1))
-                nc.vector.scalar_tensor_tensor(
-                    out=o_t[k][:, k % 2, cols],
-                    in0=w_t[k][:, k % 2, cols],
-                    scalar=KEEP,
-                    in1=st[k]["u"][c][:].rearrange("p a b -> p (a b)"),
-                    op0=ALU.mult,
-                    op1=ALU.subtract,
-                )
-                if k == TILES - 1:
-                    nc.sync.dma_start(out=out_v[:, k, cols], in_=o_t[k][:, 1, cols])
-            if k == TILES - 2:
-                nc.sync.dma_start(out=out_v[:, k, :], in_=o_t[k][:, 0, :])
-            elif k % 2 == 1 and k < TILES - 1:
-                nc.sync.dma_start(out=out_v[:, k - 1 : k + 1, :], in_=o_t[k][:])
+        def lift(k, c):
+            cols = slice(512 * c, 512 * (c + 1))
+            u = ps_u.tile([P, 4, P], F32, name="u")
+            nc.tensor.matmul_mx(
+                out=u[:].rearrange("p a b -> p (a b)"),
+                lhsT=st[k]["hc"][:].bitcast(FP8X4),
+                lhsT_scale=st[k]["hs"][:],
+                rhs=b_c[:, cols].bitcast(FP8X4),
+                rhs_scale=b_s[:, cols],
+                start=True,
+                stop=True,
+            )
+            u_bank[k, c] = u
+
+        def finish(k, c):
+            cols = slice(512 * c, 512 * (c + 1))
+            o = outp.tile([P, 512], F32, name="o")
+            nc.vector.scalar_tensor_tensor(
+                out=o[:],
+                in0=w_t[k][:, k % 2, cols],
+                scalar=KEEP,
+                in1=u_bank[k, c][:].rearrange("p a b -> p (a b)"),
+                op0=ALU.mult,
+                op1=ALU.subtract,
+            )
+            nc.sync.dma_start(out=out_v[:, k, cols], in_=o[:])
 
         for t in range(4):
             load_a(t)
         load_mom(0, 1)
+        load_b(0)
         load_v(0)
         load_mom(1, 1)
-        load_b(0)
-        load_b(1)
         load_mom(2)
+        load_b(1)
         load_w(0)
-        load_v(1)
+        load_b(2)
         load_mom(4)
+        load_v(1)
         load_w(2)
         load_mom(6)
-        load_w(4)
         load_v(2)
         load_mom(8)
-        load_w(6)
+        load_w(4)
+        more = [(load_mom, 10), (load_w, 6), (load_v, 3), (load_mom, 12), (load_w, 8), (load_mom, 14), (load_w, 10), (load_w, 12), (load_w, 14)]
 
         V_J, S_J = range(0, 8), range(8, 12)
         scale_a(0, V_J, "V")
@@ -338,53 +355,67 @@ def tile_lowrank_adam_style_step_d7_kernel(
         quant_a(0)
         quant_a(1)
         quant_a(2)
+
+        queue, outstanding = [], []
+        allowed = {0}
+
+        def next_final():
+            for x in queue:
+                if x[1] in allowed:
+                    queue.remove(x)
+                    return x
+            return None
+
+        def step(s, n, ev=(), es=(), sh=False):
+            ev, es = list(ev), list(es)
+            if sh and s + 4 < TILES:
+                shuffle(s + 4)
+            if s + 3 < TILES:
+                turn(s + 3)
+            vec = [lambda: direction(s), lambda: quant_mom(s + 2), lambda: quant_h(s), lambda: None]
+            on = [s < TILES, s + 2 < TILES, s < TILES, False]
+            for i in range(4):
+                if outstanding and (i < 3 or n > 3):
+                    finish(*outstanding.pop(0))
+                if s + 1 < TILES:
+                    project(s + 1, i)
+                if i < n:
+                    x = next_final()
+                    if x is not None:
+                        lift(*x)
+                        outstanding.append(x)
+                if on[i]:
+                    vec[i]()
+                if ev:
+                    ev.pop(0)()
+            for f in ev:
+                f()
+            if s + 3 < TILES:
+                empty(s + 3)
+            for f in es:
+                f()
+            if s < TILES:
+                queue.extend((s, c) for c in range(CHUNKS))
+            if more:
+                f, a = more.pop(0)
+                f(a)
         quant_mom(0)
-        project(0)
+        widen_b(0, 0, 4, "V")
+        for t in range(4):
+            project(0, t)
         turn(2)
-        widen_b(0, "S")
-        widen_b(1, "V")
-        widen_b(2, "V")
+        scale_b(0, (0, 1, 2, 3), "V")
         quant_mom(1)
-        project(1)
-        widen_b(3, "V")
-        empty(2)
-        scale_b(range(0, 4), "V")
-        direction(0)
-        scale_b(range(8, 10), "S")
-        quant_mom(2)
-        quant_h(0)
-        turn(3)
-        scale_b(range(4, 8), "V")
-        scale_b(range(10, 12), "S")
-        empty(3)
-        direction(1)
         quant_b(0)
-        quant_h(1)
-        quant_b(1)
-        quant_b(2)
-        lift(0)
-        project(2)
-        quant_mom(3)
-        for s in range(2, TILES + 2):
-            if s + 2 < TILES:
-                turn(s + 2)
-            finish(s - 2)
-            if s % 2 == 1:
-                if s + 7 < TILES:
-                    load_mom(s + 7)
-                if s + 5 < TILES:
-                    load_w(s + 5)
-                if s == 3:
-                    load_v(3)
-            if s + 2 < TILES:
-                empty(s + 2)
-            if s < TILES:
-                direction(s)
-            if s + 1 < TILES:
-                project(s + 1)
-            if s - 1 < TILES:
-                lift(s - 1)
-            if s + 2 < TILES:
-                quant_mom(s + 2)
-            if s < TILES:
-                quant_h(s)
+        empty(2)
+
+        step(0, 0, (lambda: widen_b(1, 0, 4, "V"), lambda: scale_b(1, (0, 1), "V")), (lambda: scale_b(1, (2, 3), "S"),))
+        step(1, 1, (lambda: quant_b(1),), (lambda: widen_b(2, 0, 4, "S"),))
+        allowed.add(1)
+        step(2, 2, (lambda: scale_b(2, (0, 1), "V"),), (lambda: scale_b(2, (2, 3), "S"),))
+        step(3, 3, (lambda: quant_b(2),))
+        allowed.add(2)
+        for s in range(4, TILES):
+            step(s, 4 if len(queue) > 4 else 3, sh=True)
+        while queue or outstanding:
+            step(TILES, 3)

from contextlib import ExitStack

import concourse.mybir as mybir
from concourse.masks import make_identity

M, N, R = 2048, 1536, 512
KEEP = 0.9

FLOPS = 2 * 2 * M * N * R

F32 = mybir.dt.float32
BF16 = mybir.dt.bfloat16
U32 = mybir.dt.uint32
U8 = mybir.dt.uint8
FP8 = mybir.dt.float8_e4m3fn
FP8X4 = mybir.dt.float8_e4m3fn_x4
ALU = mybir.AluOpType
ACT = mybir.ActivationFunctionType

P = 128
TILES = M // P
GROUPS = N // 512
ROWBLK = R // P
NBLK = N // P
CHUNKS = N // 512
A_BANKS = [("r", "r"), ("r", "r"), ("u", "u"), ("u", "u"), ("u", "u"), ("t", "bank"), ("r", "r"), ("r", "r")]


def tile_lowrank_adam_style_step_d7_kernel(
    tc, mom, v, w, a_bytes, a_scale, b_bytes, b_scale, out
):
    nc = tc.nc
    mom_v = mom.rearrange("(p i) k -> p i k", i=TILES)
    v_v = v.rearrange("(p i) r -> p i r", i=TILES)
    w_v = w.rearrange("(p i) n -> p i n", i=TILES)
    out_v = out.rearrange("(p i) n -> p i n", i=TILES)
    a_rows = a_bytes.rearrange("(p t) k -> p t k", t=4)
    b_rows = b_bytes.rearrange("(p t) n -> p t n", t=4)

    with ExitStack() as ctx:
        keep = ctx.enter_context(tc.tile_pool(name="keep", bufs=1))
        momp = ctx.enter_context(tc.tile_pool(name="momp", bufs=6))
        wp = ctx.enter_context(tc.tile_pool(name="wp", bufs=8))
        widep = ctx.enter_context(tc.tile_pool(name="widep", bufs=4))
        bp = ctx.enter_context(tc.tile_pool(name="bp", bufs=2))
        hqp = ctx.enter_context(tc.tile_pool(name="hqp", bufs=8))
        work = ctx.enter_context(tc.tile_pool(name="work", bufs=3))
        shp = ctx.enter_context(tc.tile_pool(name="shp", bufs=2))
        rsp = ctx.enter_context(tc.tile_pool(name="rsp", bufs=5))
        outp = ctx.enter_context(tc.tile_pool(name="outp", bufs=14))
        ps_tr = ctx.enter_context(tc.psum_pool(name="ps_tr", bufs=3))
        ps_r = ctx.enter_context(tc.psum_pool(name="ps_r", bufs=2))
        ps_u = ctx.enter_context(tc.psum_pool(name="ps_u", bufs=3))
        ctx.enter_context(tc.manual_schedule())

        warm = keep.tile([P, 1], F32)
        nc.vector.memset(warm[:], 1.0)
        warm_o = keep.tile([P, 1], F32)
        a_sc = keep.tile([P, NBLK], F32)
        b_sc = keep.tile([P, NBLK], F32)
        a_all = keep.tile([P, ROWBLK * NBLK], F32)
        b_all = keep.tile([P, ROWBLK * NBLK], F32)
        nc.scalar.dma_start(out=a_all[:], in_=a_scale.rearrange("i j -> (i j)").partition_broadcast(P))
        nc.scalar.dma_start(out=b_all[:], in_=b_scale.rearrange("i j -> (i j)").partition_broadcast(P))
        for q in range(4):
            rows = slice(32 * q, 32 * q + 32)
            nc.vector.tensor_copy(out=a_sc[rows], in_=a_all[rows, NBLK * q : NBLK * (q + 1)])
        nc.scalar.activation(out=warm_o[:], in_=warm[:], func=ACT.Abs_reciprocal_sqrt)
        ident = keep.tile([P, P], F32)
        make_identity(nc, ident[:])
        for q in range(4):
            rows = slice(32 * q, 32 * q + 32)
            nc.gpsimd.tensor_copy(out=b_sc[rows], in_=b_all[rows, NBLK * q : NBLK * (q + 1)])

        mom_t, v_t, w_t, o_t = {}, {}, {}, {}
        a_b = keep.tile([P, 4, N], U8)
        b_b = [keep.tile([P, 4, 512], U8, name="b_b%d" % c) for c in range(CHUNKS)]

        def load_a(t):
            nc.sync.dma_start(out=a_b[:, t, :], in_=a_rows[:, t, :])

        def load_b(c):
            nc.sync.dma_start(out=b_b[c][:], in_=b_rows[:, :, 512 * c : 512 * (c + 1)])

        def load_mom(k, n=2):
            if k % 2 == 0:
                mom_t[k] = momp.tile([P, 2, N], BF16, name="mom_t")
                mom_t[k + 1] = mom_t[k]
            h = k % 2
            nc.sync.dma_start(out=mom_t[k][:, h : h + n, :], in_=mom_v[:, k : k + n, :])

        def load_v(j):
            vt = keep.tile([P, 4, R], BF16, name="v_t%d" % j)
            nc.sync.dma_start(out=vt[:], in_=v_v[:, 4 * j : 4 * j + 4, :])
            v_t[j] = vt

        def load_w(k):
            wt = wp.tile([P, 2, N], BF16, name="w_t")
            nc.sync.dma_start(out=wt[:], in_=w_v[:, k : k + 2, :])
            w_t[k] = w_t[k + 1] = wt

        def cast(e, dst, src):
            if e == "S":
                nc.scalar.copy(out=dst, in_=src)
            else:
                nc.vector.tensor_copy(out=dst, in_=src)

        def scaled(e, dst, src, sc):
            if e == "S":
                nc.scalar.activation(out=dst, in_=src, func=ACT.Copy, scale=sc)
            else:
                nc.vector.tensor_scalar(out=dst, in0=src, scalar1=sc, scalar2=None, op0=ALU.mult)

        a_g = keep.tile([P, GROUPS, 4 * R], BF16, align_bytes=64)
        a_c = keep.tile([P, GROUPS, R], U32, align_bytes=64)
        a_s = keep.tile([P, GROUPS, R], U8, align_bytes=64)
        a_words = a_g[:].bitcast(F32).rearrange("p g (m u) -> p g m u", u=2)
        a_wide, a_bank = {}, {}

        def scale_a(t, js, e):
            if t not in a_wide:
                a_wide[t] = widep.tile([P, N], BF16, name="wide")
            for j in js:
                cols = slice(P * j, P * (j + 1))
                scaled(e, a_wide[t][:, cols], a_b[:, t, cols].bitcast(FP8), a_sc[:, j : j + 1])

        def turn_a(t, bs=(0, 1)):
            words = a_wide[t][:].bitcast(F32)
            for b in bs:
                g0, g1 = ((0, 2), (2, 3))[b]
                pool, name = A_BANKS[2 * t + b]
                bank = {"t": ps_tr, "r": ps_r, "u": ps_u}[pool].tile([P, 4, P], F32, name=name)
                a_bank[t, b] = bank
                for g in range(g0, g1):
                    for u in range(2):
                        nc.tensor.transpose(
                            bank[:, 2 * (g - g0) + u, :],
                            words[:, 256 * g + u : 256 * (g + 1) : 2],
                            ident[:],
                        )

        def empty_a(t, b, e):
            g0, g1 = ((0, 2), (2, 3))[b]
            cast(
                e,
                a_words[:, g0:g1, P * t : P * (t + 1), :],
                a_bank[t, b][:, 0 : 2 * (g1 - g0), :].rearrange("p (g u) m -> p g m u", u=2),
            )

        def quant_a(g):
            nc.vector.quantize_mx(
                out=a_c[:, g, :].bitcast(FP8X4), scales=a_s[:, g, :], in_=a_g[:, g, :]
            )

        b_c = keep.tile([P, N], U32, align_bytes=64)
        b_s = keep.tile([P, N], U8, align_bytes=64)
        b_wide, b_g = {}, {}

        def widen_b(c, t0, t1, e):
            if c not in b_wide:
                b_wide[c] = bp.tile([P, 4, 512], BF16, name="b_wide")
            cast(
                e,
                b_wide[c][:, t0:t1, :].rearrange("p t n -> p (t n)"),
                b_b[c][:, t0:t1, :].rearrange("p t n -> p (t n)").bitcast(FP8),
            )

        def scale_b(c, js, e):
            if c not in b_g:
                b_g[c] = bp.tile([P, 512, 4], BF16, align_bytes=64, name="b_g")
            for j in js:
                cols = slice(P * j, P * (j + 1))
                jj = 4 * c + j
                scaled(e, b_g[c][:, cols, :], b_wide[c][:, :, cols].rearrange("p t n -> p n t"), b_sc[:, jj : jj + 1])

        def quant_b(c):
            cols = slice(512 * c, 512 * (c + 1))
            nc.vector.quantize_mx(
                out=b_c[:, cols].bitcast(FP8X4),
                scales=b_s[:, cols],
                in_=b_g[c][:].rearrange("p n t -> p (n t)"),
            )

        st = {k: {} for k in range(TILES)}

        def shuffle(k):
            words = mom_t[k][:, k % 2, :].bitcast(F32)
            vwords = v_t[k // 4][:, k % 4, :].bitcast(F32)
            sh = shp.tile([P, 4, P], F32, name="sh")
            nc.scalar.copy(out=sh[:, 0:2, :], in_=words[:, 512:768].rearrange("p (n u) -> p u n", u=2))
            nc.scalar.copy(out=sh[:, 2:4, :], in_=vwords.rearrange("p (n u) -> p u n", u=2))
            st[k]["sh"] = sh

        def turn(k):
            words = mom_t[k][:, k % 2, :].bitcast(F32)
            vwords = v_t[k // 4][:, k % 4, :].bitcast(F32)
            bx = ps_tr.tile([P, 4, P], F32, name="bank")
            for g in range(2):
                for u in range(2):
                    nc.tensor.transpose(
                        bx[:, 2 * g + u, :], words[:, 256 * g + u : 256 * (g + 1) : 2], ident[:]
                    )
            by = ps_tr.tile([P, 4, P], F32, name="bank")
            for u in range(2):
                nc.tensor.transpose(
                    by[:, u, :], st[k]["sh"][:, u, :] if "sh" in st[k] else words[:, 512 + u : 768 : 2], ident[:]
                )
            for u in range(2):
                nc.tensor.transpose(
                    by[:, 2 + u, :], st[k]["sh"][:, 2 + u, :] if "sh" in st[k] else vwords[:, u::2], ident[:]
                )
            st[k]["bx"], st[k]["by"] = bx, by

        def empty(k):
            bx, by = st[k]["bx"], st[k]["by"]
            mg = work.tile([P, GROUPS, 4 * P], BF16, align_bytes=64, name="mg")
            mg_words = mg[:].bitcast(F32)
            nc.scalar.copy(
                out=mg_words[:, 0:2, :].rearrange("p g (n u) -> p g n u", u=2),
                in_=bx[:].rearrange("p (g u) n -> p g n u", u=2),
            )
            nc.scalar.copy(
                out=mg_words[:, 2, :].rearrange("p (n u) -> p n u", u=2),
                in_=by[:, 0:2, :].rearrange("p u n -> p n u"),
            )
            rs = rsp.tile([P, P, 2, 2], F32, name="rs")
            nc.scalar.activation(
                out=rs[:],
                in_=by[:, 2:4, :].bitcast(BF16).rearrange("p u (n e) -> p n u e", e=2),
                func=ACT.Abs_reciprocal_sqrt,
            )
            st[k]["mg"], st[k]["rs"] = mg, rs

        def quant_mom(k, parts=(0, 1)):
            mg = st[k]["mg"]
            if 0 in parts:
                st[k]["mc"] = work.tile([P, GROUPS, P], U32, align_bytes=64, name="mc")
                st[k]["ms"] = work.tile([P, GROUPS, P], U8, align_bytes=64, name="ms")
            mc, ms = st[k]["mc"], st[k]["ms"]
            for g0, g1 in [((0, 2), (2, 3))[x] for x in parts]:
                nc.vector.quantize_mx(
                    out=mc[:, g0:g1, :].rearrange("p g n -> p (g n)").bitcast(FP8X4),
                    scales=ms[:, g0:g1, :].rearrange("p g n -> p (g n)"),
                    in_=mg[:, g0:g1, :].rearrange("p g n -> p (g n)"),
                )

        def project(k, t):
            mc, ms = st[k]["mc"], st[k]["ms"]
            if t == 0:
                st[k]["r"] = ps_r.tile([P, 4, P], F32, name="r")
            for g in range(GROUPS):
                nc.tensor.matmul_mx(
                    out=st[k]["r"][:, t, :],
                    lhsT=a_c[:, g, P * t : P * (t + 1)].bitcast(FP8X4),
                    lhsT_scale=a_s[:, g, P * t : P * (t + 1)],
                    rhs=mc[:, g, :].bitcast(FP8X4),
                    rhs_scale=ms[:, g, :],
                    start=(g == 0),
                    stop=(g == GROUPS - 1),
                )

        def direction(k):
            h = work.tile([P, P, 4], BF16, align_bytes=64, name="h")
            nc.vector.tensor_tensor(
                out=h[:],
                in0=st[k]["r"][:].rearrange("p t n -> p n t"),
                in1=st[k]["rs"][:].rearrange("p n u e -> p n (u e)"),
                op=ALU.mult,
            )
            st[k]["h"] = h

        def quant_h(k):
            hc = hqp.tile([P, P], U32, align_bytes=64, name="hc")
            hs = hqp.tile([P, P], U8, align_bytes=64, name="hs")
            nc.vector.quantize_mx(
                out=hc[:].bitcast(FP8X4),
                scales=hs[:],
                in_=st[k]["h"][:].rearrange("p n t -> p (n t)"),
            )
            st[k]["hc"], st[k]["hs"] = hc, hs

        u_bank = {}

        def lift(k, c):
            cols = slice(512 * c, 512 * (c + 1))
            u = ps_u.tile([P, 4, P], F32, name="u")
            nc.tensor.matmul_mx(
                out=u[:].rearrange("p a b -> p (a b)"),
                lhsT=st[k]["hc"][:].bitcast(FP8X4),
                lhsT_scale=st[k]["hs"][:],
                rhs=b_c[:, cols].bitcast(FP8X4),
                rhs_scale=b_s[:, cols],
                start=True,
                stop=True,
            )
            u_bank[k, c] = u

        def finish(k, c):
            cols = slice(512 * c, 512 * (c + 1))
            o = outp.tile([P, 512], F32, name="o")
            nc.vector.scalar_tensor_tensor(
                out=o[:],
                in0=w_t[k][:, k % 2, cols],
                scalar=KEEP,
                in1=u_bank[k, c][:].rearrange("p a b -> p (a b)"),
                op0=ALU.mult,
                op1=ALU.subtract,
            )
            nc.sync.dma_start(out=out_v[:, k, cols], in_=o[:])

        for t in range(4):
            load_a(t)
        load_mom(0, 1)
        load_b(0)
        load_v(0)
        load_mom(1, 1)
        load_mom(2)
        load_b(1)
        load_w(0)
        load_b(2)
        load_mom(4)
        load_v(1)
        load_w(2)
        load_mom(6)
        load_v(2)
        load_mom(8)
        load_w(4)
        more = [(load_mom, 10), (load_w, 6), (load_v, 3), (load_mom, 12), (load_w, 8), (load_mom, 14), (load_w, 10), (load_w, 12), (load_w, 14)]

        V_J, S_J = range(0, 8), range(8, 12)
        scale_a(0, V_J, "V")
        scale_a(0, S_J, "S")
        turn_a(0)
        scale_a(1, V_J, "V")
        scale_a(1, S_J, "S")
        turn_a(1)
        scale_a(2, V_J, "V")
        empty_a(0, 0, "S")
        scale_a(2, S_J, "S")
        turn_a(2)
        empty_a(0, 1, "V")
        scale_a(3, V_J, "V")
        empty_a(1, 0, "S")
        scale_a(3, S_J, "S")
        turn_a(3)
        turn(0)
        empty_a(1, 1, "V")
        empty_a(2, 1, "V")
        empty_a(2, 0, "S")
        empty_a(3, 0, "V")
        empty_a(3, 1, "V")
        empty(0)
        turn(1)
        empty(1)
        quant_a(0)
        quant_a(1)
        quant_a(2)

        queue, outstanding = [], []
        allowed = {0}

        def next_final():
            for x in queue:
                if x[1] in allowed:
                    queue.remove(x)
                    return x
            return None

        def step(s, n, ev=(), es=(), sh=False):
            ev, es = list(ev), list(es)
            if sh and s + 4 < TILES:
                shuffle(s + 4)
            if s + 3 < TILES:
                turn(s + 3)
            vec = [lambda: direction(s), lambda: quant_mom(s + 2), lambda: quant_h(s), lambda: None]
            on = [s < TILES, s + 2 < TILES, s < TILES, False]
            for i in range(4):
                if outstanding and (i < 3 or n > 3):
                    finish(*outstanding.pop(0))
                if s + 1 < TILES:
                    project(s + 1, i)
                if i < n:
                    x = next_final()
                    if x is not None:
                        lift(*x)
                        outstanding.append(x)
                if on[i]:
                    vec[i]()
                if ev:
                    ev.pop(0)()
            for f in ev:
                f()
            if s + 3 < TILES:
                empty(s + 3)
            for f in es:
                f()
            if s < TILES:
                queue.extend((s, c) for c in range(CHUNKS))
            if more:
                f, a = more.pop(0)
                f(a)
        quant_mom(0)
        widen_b(0, 0, 4, "V")
        for t in range(4):
            project(0, t)
        turn(2)
        scale_b(0, (0, 1, 2, 3), "V")
        quant_mom(1)
        quant_b(0)
        empty(2)

        step(0, 0, (lambda: widen_b(1, 0, 4, "V"), lambda: scale_b(1, (0, 1), "V")), (lambda: scale_b(1, (2, 3), "S"),))
        step(1, 1, (lambda: quant_b(1),), (lambda: widen_b(2, 0, 4, "S"),))
        allowed.add(1)
        step(2, 2, (lambda: scale_b(2, (0, 1), "V"),), (lambda: scale_b(2, (2, 3), "S"),))
        step(3, 3, (lambda: quant_b(2),))
        allowed.add(2)
        for s in range(4, TILES):
            step(s, 4 if len(queue) > 4 else 3, sh=True)
        while queue or outstanding:
            step(TILES, 3)
